import numpy as np
import ml_dtypes


def mxq(x, axis, fmt="e4m3"):
    dtype, down = {"e4m3": (ml_dtypes.float8_e4m3fn, 7), "e5m2": (ml_dtypes.float8_e5m2, 14)}[fmt]
    v = np.moveaxis(np.asarray(x, np.float32).astype(ml_dtypes.bfloat16).astype(np.float64), axis, -1)
    blocks = v.reshape(v.shape[:-1] + (-1, 32))
    amax = np.abs(blocks).max(-1, keepdims=True)
    byte = np.maximum(np.where(amax > 0, np.frexp(amax)[1] - 1 + 127, 0) - down, 1)
    scale = np.exp2(byte - 127.0)
    codes = (blocks / scale).astype(np.float32).astype(dtype).astype(np.float64)
    return np.moveaxis((codes * scale).reshape(v.shape), -1, axis)


WIDE = False


def mx_kscale(k):
    if not WIDE:
        return np.ones(k)
    levels = np.array([10, -10, 5, -5, 0])
    if k % 512:
        return np.exp2(np.random.permutation(np.resize(levels, k // 32))).repeat(32)
    a = np.empty((k // 512, 16))
    for p in range(k // 512):
        a[p, :8] = np.random.permutation(np.resize(levels, 8))
        for g in range(8):
            far = levels[np.abs(levels - a[p, g]) >= 10]
            a[p, g + 8] = far[np.random.randint(len(far))]
    return np.exp2(a.ravel()).repeat(32)


def f64(x):
    return np.asarray(x).astype(np.float64)


def striped8(idx):
    return np.asarray(idx).reshape(8, -1, 16).transpose(0, 2, 1).reshape(128, -1).astype(np.uint16)


def unstriped8(offs):
    return offs.reshape(8, 16, -1).transpose(0, 2, 1).reshape(8, -1).astype(np.int64)


def pick8(x, idx, run):
    r = np.arange(len(x))
    return x[r[:, None], idx[r % (8 * run) // run]]


E2M1 = np.array([0.0, 0.5, 1.0, 1.5, 2.0, 3.0, 4.0, 6.0, -0.0, -0.5, -1.0, -1.5, -2.0, -3.0, -4.0, -6.0])


def pack_weight(w, fmt):
    k, n = w.shape
    w = f64(np.asarray(w, np.float32).astype(ml_dtypes.bfloat16)).reshape(k // 32, 32, n)
    amax = np.abs(w).max(1)
    if fmt == "e4m3":
        byte = np.frexp(amax)[1] - 1 + 127 - 7
    else:
        mant, ex = np.frexp(amax / 6.0)
        byte = np.where(mant > 0.5, ex, ex - 1) + 127
    byte = np.clip(np.where(amax > 0, byte, 1), 1, 254)
    scaled = (w * np.exp2(127.0 - byte)[:, None, :]).reshape(k, n).astype(np.float32)
    by_word = np.ascontiguousarray(scaled.reshape(k // 512, 128, 4, n).transpose(0, 1, 3, 2))
    if fmt == "e4m3":
        words = by_word.astype(ml_dtypes.float8_e4m3fn).view(np.uint8)
    else:
        c = by_word.astype(ml_dtypes.float4_e2m1fn).view(np.uint8) & 0xF
        words = (c[..., 0::2] | (c[..., 1::2] << 4)).reshape(k // 512, 128, 2 * n)
    return np.ascontiguousarray(words), np.ascontiguousarray(byte.astype(np.uint8).reshape(k // 512, 16, n))


def unpack_weight(words, scales, fmt):
    g, _, n = scales.shape
    words = np.ascontiguousarray(words).reshape(g, 128, n, -1)
    if fmt == "e4m3":
        vals = words.view(ml_dtypes.float8_e4m3fn).astype(np.float64)
    else:
        nib = np.empty((g, 128, n, 4), np.uint8)
        nib[..., 0::2] = words & 0xF
        nib[..., 1::2] = words >> 4
        vals = E2M1[nib]
    vals = vals * np.repeat(np.exp2(scales.astype(np.float64) - 127.0), 8, axis=1)[..., None]
    return vals.transpose(0, 1, 3, 2).reshape(g * 512, n)


K, T, J, B, L, N = 512, 2048, 1024, 128, 512, 512


def setup_inputs():
    n = np.random.standard_normal
    idx = np.stack([np.random.permutation(T)[:J] for _ in range(8)])
    fk = mx_kscale(K)
    fl = mx_kscale(L)
    wp = pack_weight(n((K, N)) * 1 / np.sqrt(K) * fk[:, None], "e2m1")
    bxp = pack_weight(n((L, B)) / fl[:, None], "e4m3")
    wbp = pack_weight(n((L, N)) * 1 / np.sqrt(L) * fl[:, None], "e2m1")
    return {
        "xf": (n((K, T))).astype(np.float32),
        "fk": (np.random.uniform(0.5, 2.0, (K, 1)) / fk[:, None]).astype(np.float32),
        "w_words": wp[0],
        "w_scales": wp[1],
        "bx_words": bxp[0],
        "bx_scales": bxp[1],
        "wb_words": wbp[0],
        "wb_scales": wbp[1],
        "offs": striped8(idx),
    }


def reference(xf, fk, w_words, w_scales, bx_words, bx_scales, wb_words, wb_scales, offs):
    idx = unstriped8(offs)
    wu = unpack_weight(w_words, w_scales, "e2m1")
    bxu = unpack_weight(bx_words, bx_scales, "e4m3")
    wbu = unpack_weight(wb_words, wb_scales, "e2m1")
    u = pick8(f64(xf), idx, 64).reshape(K, B, J // B).max(axis=2) * f64(fk)
    uq = mxq(u, 0, "e4m3")
    y = wu.T @ uq + wbu.T @ bxu
    return y

@@ -1,0 +1,177 @@
+from contextlib import ExitStack
+
+import concourse.mybir as mybir
+
+K, T, J, B, N = 512, 2048, 1024, 128, 512
+P = 128
+PACK = 4
+BUNDLE = J // B
+FLOPS = 2 * 2 * K * N * B
+
+F32 = mybir.dt.float32
+BF16 = mybir.dt.bfloat16
+I32 = mybir.dt.int32
+U32 = mybir.dt.uint32
+U16 = mybir.dt.uint16
+U8 = mybir.dt.uint8
+FP8X4 = mybir.dt.float8_e4m3fn_x4
+FP4X4 = mybir.dt.float4_e2m1fn_x4
+ALU = mybir.AluOpType
+ACT = mybir.ActivationFunctionType
+
+
+def load_scales(nc, plane, scales):
+    for q in range(4):
+        nc.sync.dma_start(
+            out=plane[32 * q : 32 * q + 4, :].bitcast(I32),
+            in_=scales[0, 4 * q : 4 * q + 4, :].bitcast(I32),
+        )
+
+
+def tile_moe_expert_heads_bundled_kernel(
+    tc, xf, fk, w_words, w_scales, bx_words, bx_scales, wb_words, wb_scales, offs, out
+):
+    nc = tc.nc
+    with ExitStack() as ctx:
+        keep = ctx.enter_context(tc.tile_pool(name="keep", bufs=1))
+        psum = ctx.enter_context(tc.psum_pool(name="psum", bufs=1))
+
+        offsets = keep.tile([P, J // 16], U16, name="offsets")
+        windows = [keep.tile([P, T], F32, name=f"window{t}") for t in range(PACK)]
+        rows = xf.rearrange("(p t) w -> p t w", t=PACK)
+        nc.sync.dma_start(out=windows[0][:], in_=rows[:, 0, :])
+        nc.sync.dma_start(offsets[:], offs)
+        for t in range(1, PACK):
+            nc.sync.dma_start(out=windows[t][:], in_=rows[:, t, :])
+        factor = keep.tile([P, PACK], F32, name="factor")
+        nc.scalar.dma_start(out=factor[:], in_=fk.rearrange("(p t) o -> p (t o)", t=PACK))
+
+        w_codes = keep.tile([P, 2 * N], U8, name="w_codes", align_bytes=64)
+        wb_codes = keep.tile([P, 2 * N], U8, name="wb_codes", align_bytes=64)
+        bx_codes = keep.tile([P, 4 * B], U8, name="bx_codes", align_bytes=64)
+        w_plane = keep.tile([P, N], U8, name="w_plane", align_bytes=64)
+        wb_plane = keep.tile([P, N], U8, name="wb_plane", align_bytes=64)
+        bx_plane = keep.tile([P, B], U8, name="bx_plane", align_bytes=64)
+        for plane in (wb_plane, bx_plane, w_plane):
+            nc.vector.memset(plane[:].bitcast(I32), 0)
+        nc.sync.dma_start(out=wb_codes[:].bitcast(I32), in_=wb_words[0].bitcast(I32))
+        nc.sync.dma_start(
+            out=bx_codes[:].bitcast(I32),
+            in_=bx_words[0].rearrange("p c r -> p (c r)").bitcast(I32),
+        )
+        nc.sync.dma_start(out=w_codes[:].bitcast(I32), in_=w_words[0].bitcast(I32))
+        load_scales(nc, wb_plane, wb_scales)
+        load_scales(nc, bx_plane, bx_scales)
+        load_scales(nc, w_plane, w_scales)
+
+        banks = [psum.tile([P, B], F32, name=f"bank{g}") for g in range(N // P)]
+        for g in range(N // P):
+            nc.tensor.matmul_mx(
+                out=banks[g][:],
+                lhsT=wb_codes[:, 2 * P * g : 2 * P * (g + 1)].bitcast(FP4X4),
+                lhsT_scale=wb_plane[:, P * g : P * (g + 1)],
+                rhs=bx_codes[:].bitcast(FP8X4),
+                rhs_scale=bx_plane[:],
+                start=True,
+                stop=False,
+            )
+
+        size = keep.tile([P, PACK], F32, name="size")
+        sign = keep.tile([P, PACK], F32, name="sign")
+        nc.scalar.activation(out=size[:], in_=factor[:], func=ACT.Abs)
+        nc.scalar.activation(out=sign[:], in_=factor[:], func=ACT.Sign)
+
+        slots = J // 2
+        bundles = B // 2
+        pieces = 2 * PACK
+        picked = [keep.tile([P, slots], F32, name=f"picked{i}") for i in range(pieces)]
+        u = keep.tile([P, B, PACK], BF16, name="u", align_bytes=64)
+
+        def gather(i):
+            cols = slice((i % 2) * slots // 16, (i % 2 + 1) * slots // 16)
+            nc.vector.tensor_copy(picked[i][:], windows[i // 2][:].indirect(offsets[:, cols]))
+
+        def scale(i, dst):
+            t = i // 2
+            nc.scalar.activation(
+                out=dst.rearrange("p (c r e) -> p c r e", r=BUNDLE, e=2),
+                in_=picked[i][:].rearrange("p (c e r) -> p c r e", r=BUNDLE, e=2),
+                func=ACT.Copy,
+                scale=size[:, t : t + 1],
+            )
+
+        def halve(dst, src, width, cs):
+            s = src.rearrange("p n (c h w) -> p n c h w", h=2, w=width)
+            d = dst.rearrange("p n (c w) -> p n c w", w=width)
+            nc.vector.tensor_tensor(out=d[:, :, cs, :], in0=s[:, :, cs, 0, :], in1=s[:, :, cs, 1, :], op=ALU.max)
+
+        def place(src, t, b0, b1, by):
+            nc.scalar.activation(out=u[:, b0:b1, t], in_=src, func=ACT.Copy, scale=by[:, t : t + 1])
+
+        early, late = 5, 2
+        a8 = keep.tile([P, early, slots], BF16, name="a8")
+        a4 = keep.tile([P, early, slots // 2], BF16, name="a4")
+        a2 = keep.tile([P, early, slots // 4], BF16, name="a2")
+        a1 = keep.tile([P, early, slots // 8], BF16, name="a1")
+        b8 = keep.tile([P, late, slots], BF16, name="b8")
+        b4 = keep.tile([P, late, slots // 2], BF16, name="b4")
+        b2 = keep.tile([P, late, slots // 4], BF16, name="b2")
+        b1 = keep.tile([P, late, slots // 8], BF16, name="b1")
+
+        for i in range(early):
+            gather(i)
+            scale(i, a8[:, i, :])
+        gather(early)
+        scale(early, b8[:, 0, :])
+        pairs = bundles // 2
+        for dst, src, width in ((a4, a8, 8), (a2, a4, 4), (a1, a2, 2)):
+            for cs in (slice(0, pairs // 2), slice(pairs // 2, pairs)):
+                halve(dst[:], src[:], width, cs)
+        for t in range(2):
+            place(a1[:, 2 * t : 2 * t + 2, :].rearrange("p n b -> p (n b)"), t, 0, B, sign)
+        place(a1[:, 4, :], 2, 0, bundles, sign)
+
+        gather(6)
+        scale(6, b8[:, 1, :])
+        gather(7)
+
+        def reduce(lo, hi):
+            nc.vector.tensor_reduce(
+                out=picked[6][:, lo:hi],
+                in_=picked[7][:, lo * BUNDLE : hi * BUNDLE].rearrange("p (b r) -> p b r", r=BUNDLE),
+                axis=mybir.AxisListType.X,
+                op=ALU.max,
+            )
+            place(picked[6][:, lo:hi], 3, bundles + lo, bundles + hi, factor)
+
+        halve(b4[:], b8[:], 8, slice(0, pairs))
+        reduce(0, bundles // 2)
+        halve(b2[:], b4[:], 4, slice(0, pairs))
+        halve(b1[:], b2[:], 2, slice(0, pairs))
+        place(b1[:, 0, :], 2, bundles, B, sign)
+        place(b1[:, 1, :], 3, 0, bundles, sign)
+        reduce(bundles // 2, bundles)
+
+        u_codes = keep.tile([P, B], U32, name="u_codes", align_bytes=64)
+        u_plane = keep.tile([P, B], U8, name="u_plane", align_bytes=64)
+        nc.vector.quantize_mx(
+            out=u_codes[:].bitcast(FP8X4), scales=u_plane[:], in_=u[:].rearrange("p b t -> p (b t)")
+        )
+
+        for g in range(N // P):
+            nc.tensor.matmul_mx(
+                out=banks[g][:],
+                lhsT=w_codes[:, 2 * P * g : 2 * P * (g + 1)].bitcast(FP4X4),
+                lhsT_scale=w_plane[:, P * g : P * (g + 1)],
+                rhs=u_codes[:].bitcast(FP8X4),
+                rhs_scale=u_plane[:],
+                start=False,
+                stop=True,
+            )
+            result = keep.tile([P, B], F32, name=f"result{g}")
+            if g % 2 == 0:
+                nc.vector.tensor_copy(out=result[:], in_=banks[g][:])
+                nc.sync.dma_start(out=out[P * g : P * (g + 1), :], in_=result[:])
+            else:
+                nc.scalar.copy(out=result[:], in_=banks[g][:])
+                nc.scalar.dma_start(out=out[P * g : P * (g + 1), :], in_=result[:])

@@ -20,8 +20,8 @@ ALU = mybir.AluOpType
 ACT = mybir.ActivationFunctionType
 
 
-def load_scales(nc, plane, scales):
-    for q in range(4):
+def load_scales(nc, plane, scales, quadrants):
+    for q in quadrants:
         nc.sync.dma_start(
             out=plane[32 * q : 32 * q + 4, :].bitcast(I32),
             in_=scales[0, 4 * q : 4 * q + 4, :].bitcast(I32),
@@ -39,30 +39,30 @@ def tile_moe_expert_heads_bundled_kernel(
         offsets = keep.tile([P, J // 16], U16, name="offsets")
         windows = [keep.tile([P, T], F32, name=f"window{t}") for t in range(PACK)]
         rows = xf.rearrange("(p t) w -> p t w", t=PACK)
-        nc.sync.dma_start(out=windows[0][:], in_=rows[:, 0, :])
-        nc.sync.dma_start(offsets[:], offs)
-        for t in range(1, PACK):
-            nc.sync.dma_start(out=windows[t][:], in_=rows[:, t, :])
         factor = keep.tile([P, PACK], F32, name="factor")
-        nc.scalar.dma_start(out=factor[:], in_=fk.rearrange("(p t) o -> p (t o)", t=PACK))
-
         w_codes = keep.tile([P, 2 * N], U8, name="w_codes", align_bytes=64)
         wb_codes = keep.tile([P, 2 * N], U8, name="wb_codes", align_bytes=64)
         bx_codes = keep.tile([P, 4 * B], U8, name="bx_codes", align_bytes=64)
         w_plane = keep.tile([P, N], U8, name="w_plane", align_bytes=64)
         wb_plane = keep.tile([P, N], U8, name="wb_plane", align_bytes=64)
         bx_plane = keep.tile([P, B], U8, name="bx_plane", align_bytes=64)
-        for plane in (wb_plane, bx_plane, w_plane):
-            nc.vector.memset(plane[:].bitcast(I32), 0)
+
+        nc.sync.dma_start(out=windows[0][:], in_=rows[:, 0, :])
+        nc.sync.dma_start(offsets[:], offs)
+        nc.scalar.dma_start(out=factor[:], in_=fk.rearrange("(p t) o -> p (t o)", t=PACK))
+        nc.sync.dma_start(out=windows[1][:], in_=rows[:, 1, :])
+        nc.sync.dma_start(out=windows[2][:], in_=rows[:, 2, :])
+        load_scales(nc, wb_plane, wb_scales, range(4))
+        load_scales(nc, bx_plane, bx_scales, range(2))
+        nc.sync.dma_start(out=windows[3][:], in_=rows[:, 3, :])
         nc.sync.dma_start(out=wb_codes[:].bitcast(I32), in_=wb_words[0].bitcast(I32))
         nc.sync.dma_start(
             out=bx_codes[:].bitcast(I32),
             in_=bx_words[0].rearrange("p c r -> p (c r)").bitcast(I32),
         )
         nc.sync.dma_start(out=w_codes[:].bitcast(I32), in_=w_words[0].bitcast(I32))
-        load_scales(nc, wb_plane, wb_scales)
-        load_scales(nc, bx_plane, bx_scales)
-        load_scales(nc, w_plane, w_scales)
+        load_scales(nc, bx_plane, bx_scales, range(2, 4))
+        load_scales(nc, w_plane, w_scales, range(4))
 
         banks = [psum.tile([P, B], F32, name=f"bank{g}") for g in range(N // P)]
         for g in range(N // P):
@@ -83,74 +83,83 @@ def tile_moe_expert_heads_bundled_kernel(
 
         slots = J // 2
         bundles = B // 2
-        pieces = 2 * PACK
-        picked = [keep.tile([P, slots], F32, name=f"picked{i}") for i in range(pieces)]
+        pairs = bundles // 2
         u = keep.tile([P, B, PACK], BF16, name="u", align_bytes=64)
 
-        def gather(i):
-            cols = slice((i % 2) * slots // 16, (i % 2 + 1) * slots // 16)
-            nc.vector.tensor_copy(picked[i][:], windows[i // 2][:].indirect(offsets[:, cols]))
+        def gather(t, lo, hi):
+            picked = keep.tile([P, hi - lo], F32, name=f"picked{t}_{lo}")
+            nc.vector.tensor_copy(picked[:], windows[t][:].indirect(offsets[:, lo // 16 : hi // 16]))
+            return picked
 
-        def scale(i, dst):
-            t = i // 2
+        def scale(dst, picked, t):
             nc.scalar.activation(
                 out=dst.rearrange("p (c r e) -> p c r e", r=BUNDLE, e=2),
-                in_=picked[i][:].rearrange("p (c e r) -> p c r e", r=BUNDLE, e=2),
+                in_=picked[:].rearrange("p (c e r) -> p c r e", r=BUNDLE, e=2),
                 func=ACT.Copy,
                 scale=size[:, t : t + 1],
             )
 
-        def halve(dst, src, width, cs):
-            s = src.rearrange("p n (c h w) -> p n c h w", h=2, w=width)
-            d = dst.rearrange("p n (c w) -> p n c w", w=width)
-            nc.vector.tensor_tensor(out=d[:, :, cs, :], in0=s[:, :, cs, 0, :], in1=s[:, :, cs, 1, :], op=ALU.max)
+        def halve(dst, src, width):
+            s = src.rearrange("p (c h w) -> p c h w", h=2, w=width)
+            d = dst.rearrange("p (c w) -> p c w", w=width)
+            nc.vector.tensor_tensor(out=d, in0=s[:, :, 0, :], in1=s[:, :, 1, :], op=ALU.max)
 
         def place(src, t, b0, b1, by):
             nc.scalar.activation(out=u[:, b0:b1, t], in_=src, func=ACT.Copy, scale=by[:, t : t + 1])
 
-        early, late = 5, 2
-        a8 = keep.tile([P, early, slots], BF16, name="a8")
-        a4 = keep.tile([P, early, slots // 2], BF16, name="a4")
-        a2 = keep.tile([P, early, slots // 4], BF16, name="a2")
-        a1 = keep.tile([P, early, slots // 8], BF16, name="a1")
-        b8 = keep.tile([P, late, slots], BF16, name="b8")
-        b4 = keep.tile([P, late, slots // 2], BF16, name="b4")
-        b2 = keep.tile([P, late, slots // 4], BF16, name="b2")
-        b1 = keep.tile([P, late, slots // 8], BF16, name="b1")
+        na = 5 * slots
+        a8 = keep.tile([P, na], BF16, name="a8")
+        a4 = keep.tile([P, na // 2], BF16, name="a4")
+        a2 = keep.tile([P, na // 4], BF16, name="a2")
+        a1 = keep.tile([P, na // 8], BF16, name="a1")
+        y8, y4, y2 = [keep.tile([P, slots // d], BF16, name=f"y{d}") for d in (1, 2, 4)]
+        z8, z4, z2, z1 = [keep.tile([P, slots // d], BF16, name=f"z{d}") for d in (1, 2, 4, 8)]
 
-        for i in range(early):
-            gather(i)
-            scale(i, a8[:, i, :])
-        gather(early)
-        scale(early, b8[:, 0, :])
-        pairs = bundles // 2
-        for dst, src, width in ((a4, a8, 8), (a2, a4, 4), (a1, a2, 2)):
-            for cs in (slice(0, pairs // 2), slice(pairs // 2, pairs)):
-                halve(dst[:], src[:], width, cs)
+        def view(tile, half):
+            return tile[:].rearrange("p (n h x) -> p n h x", n=5, h=2)[:, :, half, :]
+
+        def halve_a(dst, src, width, half):
+            s = view(src, half).rearrange("p n (c h w) -> p n c h w", h=2, w=width)
+            d = view(dst, half).rearrange("p n (c w) -> p n c w", w=width)
+            nc.vector.tensor_tensor(out=d, in0=s[:, :, :, 0, :], in1=s[:, :, :, 1, :], op=ALU.max)
+
         for t in range(2):
-            place(a1[:, 2 * t : 2 * t + 2, :].rearrange("p n b -> p (n b)"), t, 0, B, sign)
-        place(a1[:, 4, :], 2, 0, bundles, sign)
+            scale(a8[:, t * J : (t + 1) * J], gather(t, 0, J), t)
+        scale(a8[:, 2 * J :], gather(2, 0, slots), 2)
+        scale(y8[:], gather(2, slots, J), 2)
+        halve_a(a4, a8, 8, 0)
+        halve_a(a4, a8, 8, 1)
+        halve_a(a2, a4, 4, 0)
+        halve(y4[:], y8[:], 8)
+        halve_a(a2, a4, 4, 1)
+        halve_a(a1, a2, 2, 0)
+        halve(y2[:], y4[:], 4)
+        halve_a(a1, a2, 2, 1)
+        for t in range(2):
+            place(a1[:, t * B : (t + 1) * B], t, 0, B, sign)
+        place(a1[:, 2 * B :], 2, 0, bundles, sign)
 
-        gather(6)
-        scale(6, b8[:, 1, :])
-        gather(7)
+        first = gather(3, 0, slots)
+        scale(z8[:], first, 3)
+        last = gather(3, slots, J)
 
         def reduce(lo, hi):
             nc.vector.tensor_reduce(
-                out=picked[6][:, lo:hi],
-                in_=picked[7][:, lo * BUNDLE : hi * BUNDLE].rearrange("p (b r) -> p b r", r=BUNDLE),
+                out=first[:, lo:hi],
+                in_=last[:, lo * BUNDLE : hi * BUNDLE].rearrange("p (b r) -> p b r", r=BUNDLE),
                 axis=mybir.AxisListType.X,
                 op=ALU.max,
             )
-            place(picked[6][:, lo:hi], 3, bundles + lo, bundles + hi, factor)
+            place(first[:, lo:hi], 3, bundles + lo, bundles + hi, factor)
 
-        halve(b4[:], b8[:], 8, slice(0, pairs))
-        reduce(0, bundles // 2)
-        halve(b2[:], b4[:], 4, slice(0, pairs))
-        halve(b1[:], b2[:], 2, slice(0, pairs))
-        place(b1[:, 0, :], 2, bundles, B, sign)
-        place(b1[:, 1, :], 3, 0, bundles, sign)
-        reduce(bundles // 2, bundles)
+        halve(z4[:], z8[:], 8)
+        halve(first[:, bundles : 2 * bundles], y2[:], 2)
+        place(first[:, bundles : 2 * bundles], 2, bundles, B, sign)
+        reduce(0, pairs)
+        halve(z2[:], z4[:], 4)
+        reduce(pairs, bundles)
+        halve(z1[:], z2[:], 2)
+        place(z1[:], 3, 0, bundles, sign)
 
         u_codes = keep.tile([P, B], U32, name="u_codes", align_bytes=64)
         u_plane = keep.tile([P, B], U8, name="u_plane", align_bytes=64)

@@ -6,6 +6,10 @@ K, T, J, B, N = 512, 2048, 1024, 128, 512
 P = 128
 PACK = 4
 BUNDLE = J // B
+HALF_J = J // 2
+HALF_B = B // 2
+PER_COLUMN = 16
+QUADRANTS = 4
 FLOPS = 2 * 2 * K * N * B
 
 F32 = mybir.dt.float32
@@ -20,10 +24,10 @@ ALU = mybir.AluOpType
 ACT = mybir.ActivationFunctionType
 
 
-def load_scales(nc, plane, scales, quadrants):
+def load_scales(nc, tile, scales, quadrants):
     for q in quadrants:
         nc.sync.dma_start(
-            out=plane[32 * q : 32 * q + 4, :].bitcast(I32),
+            out=tile[32 * q : 32 * q + 4, :].bitcast(I32),
             in_=scales[0, 4 * q : 4 * q + 4, :].bitcast(I32),
         )
 
@@ -36,24 +40,24 @@ def tile_moe_expert_heads_bundled_kernel(
         keep = ctx.enter_context(tc.tile_pool(name="keep", bufs=1))
         psum = ctx.enter_context(tc.psum_pool(name="psum", bufs=1))
 
-        offsets = keep.tile([P, J // 16], U16, name="offsets")
+        offsets = keep.tile([P, J // PER_COLUMN], U16, name="offsets")
         windows = [keep.tile([P, T], F32, name=f"window{t}") for t in range(PACK)]
-        rows = xf.rearrange("(p t) w -> p t w", t=PACK)
         factor = keep.tile([P, PACK], F32, name="factor")
         w_codes = keep.tile([P, 2 * N], U8, name="w_codes", align_bytes=64)
         wb_codes = keep.tile([P, 2 * N], U8, name="wb_codes", align_bytes=64)
-        bx_codes = keep.tile([P, 4 * B], U8, name="bx_codes", align_bytes=64)
-        w_plane = keep.tile([P, N], U8, name="w_plane", align_bytes=64)
-        wb_plane = keep.tile([P, N], U8, name="wb_plane", align_bytes=64)
-        bx_plane = keep.tile([P, B], U8, name="bx_plane", align_bytes=64)
+        bx_codes = keep.tile([P, PACK * B], U8, name="bx_codes", align_bytes=64)
+        w_scale = keep.tile([P, N], U8, name="w_scale", align_bytes=64)
+        wb_scale = keep.tile([P, N], U8, name="wb_scale", align_bytes=64)
+        bx_scale = keep.tile([P, B], U8, name="bx_scale", align_bytes=64)
 
+        rows = xf.rearrange("(p t) w -> p t w", t=PACK)
         nc.sync.dma_start(out=windows[0][:], in_=rows[:, 0, :])
         nc.sync.dma_start(offsets[:], offs)
-        nc.scalar.dma_start(out=factor[:], in_=fk.rearrange("(p t) o -> p (t o)", t=PACK))
         nc.sync.dma_start(out=windows[1][:], in_=rows[:, 1, :])
+        nc.sync.dma_start(out=factor[:], in_=fk.rearrange("(p t) o -> p (t o)", t=PACK))
         nc.sync.dma_start(out=windows[2][:], in_=rows[:, 2, :])
-        load_scales(nc, wb_plane, wb_scales, range(4))
-        load_scales(nc, bx_plane, bx_scales, range(2))
+        load_scales(nc, wb_scale, wb_scales, range(QUADRANTS))
+        load_scales(nc, bx_scale, bx_scales, range(QUADRANTS // 2))
         nc.sync.dma_start(out=windows[3][:], in_=rows[:, 3, :])
         nc.sync.dma_start(out=wb_codes[:].bitcast(I32), in_=wb_words[0].bitcast(I32))
         nc.sync.dma_start(
@@ -61,17 +65,17 @@ def tile_moe_expert_heads_bundled_kernel(
             in_=bx_words[0].rearrange("p c r -> p (c r)").bitcast(I32),
         )
         nc.sync.dma_start(out=w_codes[:].bitcast(I32), in_=w_words[0].bitcast(I32))
-        load_scales(nc, bx_plane, bx_scales, range(2, 4))
-        load_scales(nc, w_plane, w_scales, range(4))
+        load_scales(nc, bx_scale, bx_scales, range(QUADRANTS // 2, QUADRANTS))
+        load_scales(nc, w_scale, w_scales, range(QUADRANTS))
 
         banks = [psum.tile([P, B], F32, name=f"bank{g}") for g in range(N // P)]
         for g in range(N // P):
             nc.tensor.matmul_mx(
                 out=banks[g][:],
                 lhsT=wb_codes[:, 2 * P * g : 2 * P * (g + 1)].bitcast(FP4X4),
-                lhsT_scale=wb_plane[:, P * g : P * (g + 1)],
+                lhsT_scale=wb_scale[:, P * g : P * (g + 1)],
                 rhs=bx_codes[:].bitcast(FP8X4),
-                rhs_scale=bx_plane[:],
+                rhs_scale=bx_scale[:],
                 start=True,
                 stop=False,
             )
@@ -81,14 +85,12 @@ def tile_moe_expert_heads_bundled_kernel(
         nc.scalar.activation(out=size[:], in_=factor[:], func=ACT.Abs)
         nc.scalar.activation(out=sign[:], in_=factor[:], func=ACT.Sign)
 
-        slots = J // 2
-        bundles = B // 2
-        pairs = bundles // 2
         u = keep.tile([P, B, PACK], BF16, name="u", align_bytes=64)
 
         def gather(t, lo, hi):
             picked = keep.tile([P, hi - lo], F32, name=f"picked{t}_{lo}")
-            nc.vector.tensor_copy(picked[:], windows[t][:].indirect(offsets[:, lo // 16 : hi // 16]))
+            entries = offsets[:, lo // PER_COLUMN : hi // PER_COLUMN]
+            nc.vector.tensor_copy(picked[:], windows[t][:].indirect(entries))
             return picked
 
         def scale(dst, picked, t):
@@ -99,81 +101,83 @@ def tile_moe_expert_heads_bundled_kernel(
                 scale=size[:, t : t + 1],
             )
 
-        def halve(dst, src, width):
-            s = src.rearrange("p (c h w) -> p c h w", h=2, w=width)
-            d = dst.rearrange("p (c w) -> p c w", w=width)
+        def halve(dst, src, run):
+            s = src.rearrange("p (c h w) -> p c h w", h=2, w=run)
+            d = dst.rearrange("p (c w) -> p c w", w=run)
             nc.vector.tensor_tensor(out=d, in0=s[:, :, 0, :], in1=s[:, :, 1, :], op=ALU.max)
 
-        def place(src, t, b0, b1, by):
-            nc.scalar.activation(out=u[:, b0:b1, t], in_=src, func=ACT.Copy, scale=by[:, t : t + 1])
+        def place(src, t, b0, by):
+            width = src.shape[1]
+            nc.scalar.activation(out=u[:, b0 : b0 + width, t], in_=src, func=ACT.Copy, scale=by[:, t : t + 1])
 
-        na = 5 * slots
-        a8 = keep.tile([P, na], BF16, name="a8")
-        a4 = keep.tile([P, na // 2], BF16, name="a4")
-        a2 = keep.tile([P, na // 4], BF16, name="a2")
-        a1 = keep.tile([P, na // 8], BF16, name="a1")
-        y8, y4, y2 = [keep.tile([P, slots // d], BF16, name=f"y{d}") for d in (1, 2, 4)]
-        z8, z4, z2, z1 = [keep.tile([P, slots // d], BF16, name=f"z{d}") for d in (1, 2, 4, 8)]
+        def levels(label, slots, count):
+            return [keep.tile([P, slots >> i], BF16, name=f"{label}{BUNDLE >> i}") for i in range(count)]
 
-        def view(tile, half):
-            return tile[:].rearrange("p (n h x) -> p n h x", n=5, h=2)[:, :, half, :]
+        half_lists = 5
+        early8, early4, early2, early1 = levels("early", half_lists * HALF_J, 4)
+        mid8, mid4, mid2 = levels("mid", HALF_J, 3)
+        late8, late4, late2, late1 = levels("late", HALF_J, 4)
 
-        def halve_a(dst, src, width, half):
-            s = view(src, half).rearrange("p n (c h w) -> p n c h w", h=2, w=width)
-            d = view(dst, half).rearrange("p n (c w) -> p n c w", w=width)
+        def halve_early(dst, src, run, part):
+            s = src[:].rearrange("p (n g c h w) -> p n g c h w", n=half_lists, g=2, h=2, w=run)[:, :, part]
+            d = dst[:].rearrange("p (n g c w) -> p n g c w", n=half_lists, g=2, w=run)[:, :, part]
             nc.vector.tensor_tensor(out=d, in0=s[:, :, :, 0, :], in1=s[:, :, :, 1, :], op=ALU.max)
 
         for t in range(2):
-            scale(a8[:, t * J : (t + 1) * J], gather(t, 0, J), t)
-        scale(a8[:, 2 * J :], gather(2, 0, slots), 2)
-        scale(y8[:], gather(2, slots, J), 2)
-        halve_a(a4, a8, 8, 0)
-        halve_a(a4, a8, 8, 1)
-        halve_a(a2, a4, 4, 0)
-        halve(y4[:], y8[:], 8)
-        halve_a(a2, a4, 4, 1)
-        halve_a(a1, a2, 2, 0)
-        halve(y2[:], y4[:], 4)
-        halve_a(a1, a2, 2, 1)
+            scale(early8[:, t * J : (t + 1) * J], gather(t, 0, J), t)
+        scale(early8[:, 2 * J :], gather(2, 0, HALF_J), 2)
+        scale(mid8[:], gather(2, HALF_J, J), 2)
+
+        halve_early(early4, early8, 8, 0)
+        halve_early(early4, early8, 8, 1)
+        halve_early(early2, early4, 4, 0)
+        halve(mid4[:], mid8[:], 8)
+        halve_early(early2, early4, 4, 1)
+        halve_early(early1, early2, 2, 0)
+        halve(mid2[:], mid4[:], 4)
+        halve_early(early1, early2, 2, 1)
         for t in range(2):
-            place(a1[:, t * B : (t + 1) * B], t, 0, B, sign)
-        place(a1[:, 2 * B :], 2, 0, bundles, sign)
+            place(early1[:, t * B : (t + 1) * B], t, 0, sign)
+        place(early1[:, 2 * B :], 2, 0, sign)
 
-        first = gather(3, 0, slots)
-        scale(z8[:], first, 3)
-        last = gather(3, slots, J)
+        first = gather(3, 0, HALF_J)
+        scale(late8[:], first, 3)
+        last = gather(3, HALF_J, J)
 
-        def reduce(lo, hi):
+        last1 = first[:, :HALF_B]
+        mid1 = first[:, HALF_B:B]
+
+        def reduce_last(lo, hi):
             nc.vector.tensor_reduce(
-                out=first[:, lo:hi],
+                out=last1[:, lo:hi],
                 in_=last[:, lo * BUNDLE : hi * BUNDLE].rearrange("p (b r) -> p b r", r=BUNDLE),
                 axis=mybir.AxisListType.X,
                 op=ALU.max,
             )
-            place(first[:, lo:hi], 3, bundles + lo, bundles + hi, factor)
+            place(last1[:, lo:hi], 3, HALF_B + lo, factor)
 
-        halve(z4[:], z8[:], 8)
-        halve(first[:, bundles : 2 * bundles], y2[:], 2)
-        place(first[:, bundles : 2 * bundles], 2, bundles, B, sign)
-        reduce(0, pairs)
-        halve(z2[:], z4[:], 4)
-        reduce(pairs, bundles)
-        halve(z1[:], z2[:], 2)
-        place(z1[:], 3, 0, bundles, sign)
+        halve(late4[:], late8[:], 8)
+        halve(mid1, mid2[:], 2)
+        place(mid1, 2, HALF_B, sign)
+        reduce_last(0, HALF_B // 2)
+        halve(late2[:], late4[:], 4)
+        reduce_last(HALF_B // 2, HALF_B)
+        halve(late1[:], late2[:], 2)
+        place(late1[:], 3, 0, sign)
 
         u_codes = keep.tile([P, B], U32, name="u_codes", align_bytes=64)
-        u_plane = keep.tile([P, B], U8, name="u_plane", align_bytes=64)
+        u_scale = keep.tile([P, B], U8, name="u_scale", align_bytes=64)
         nc.vector.quantize_mx(
-            out=u_codes[:].bitcast(FP8X4), scales=u_plane[:], in_=u[:].rearrange("p b t -> p (b t)")
+            out=u_codes[:].bitcast(FP8X4), scales=u_scale[:], in_=u[:].rearrange("p b t -> p (b t)")
         )
 
         for g in range(N // P):
             nc.tensor.matmul_mx(
                 out=banks[g][:],
                 lhsT=w_codes[:, 2 * P * g : 2 * P * (g + 1)].bitcast(FP4X4),
-                lhsT_scale=w_plane[:, P * g : P * (g + 1)],
+                lhsT_scale=w_scale[:, P * g : P * (g + 1)],
                 rhs=u_codes[:].bitcast(FP8X4),
-                rhs_scale=u_plane[:],
+                rhs_scale=u_scale[:],
                 start=False,
                 stop=True,
             )

@@ -1,6 +1,7 @@
 from contextlib import ExitStack
 
 import concourse.mybir as mybir
+from concourse.masks import make_identity
 
 K, T, J, B, N = 512, 2048, 1024, 128, 512
 P = 128
@@ -42,7 +43,7 @@ def tile_moe_expert_heads_bundled_kernel(
 
         offsets = keep.tile([P, J // PER_COLUMN], U16, name="offsets")
         windows = [keep.tile([P, T], F32, name=f"window{t}") for t in range(PACK)]
-        factor = keep.tile([P, PACK], F32, name="factor")
+        fk_row = keep.tile([P, K], F32, name="fk_row")
         w_codes = keep.tile([P, 2 * N], U8, name="w_codes", align_bytes=64)
         wb_codes = keep.tile([P, 2 * N], U8, name="wb_codes", align_bytes=64)
         bx_codes = keep.tile([P, PACK * B], U8, name="bx_codes", align_bytes=64)
@@ -50,11 +51,14 @@ def tile_moe_expert_heads_bundled_kernel(
         wb_scale = keep.tile([P, N], U8, name="wb_scale", align_bytes=64)
         bx_scale = keep.tile([P, B], U8, name="bx_scale", align_bytes=64)
 
+        fk_at = P - 1
+        nc.scalar.dma_start(out=fk_row[fk_at:, :], in_=fk.rearrange("k o -> o k"))
+        nc.vector.memset(fk_row[:fk_at, :], 0.0)
+
         rows = xf.rearrange("(p t) w -> p t w", t=PACK)
         nc.sync.dma_start(out=windows[0][:], in_=rows[:, 0, :])
         nc.sync.dma_start(offsets[:], offs)
         nc.sync.dma_start(out=windows[1][:], in_=rows[:, 1, :])
-        nc.sync.dma_start(out=factor[:], in_=fk.rearrange("(p t) o -> p (t o)", t=PACK))
         nc.sync.dma_start(out=windows[2][:], in_=rows[:, 2, :])
         load_scales(nc, wb_scale, wb_scales, range(QUADRANTS))
         load_scales(nc, bx_scale, bx_scales, range(QUADRANTS // 2))
@@ -68,6 +72,19 @@ def tile_moe_expert_heads_bundled_kernel(
         load_scales(nc, bx_scale, bx_scales, range(QUADRANTS // 2, QUADRANTS))
         load_scales(nc, w_scale, w_scales, range(QUADRANTS))
 
+        identity = keep.tile([P, P], F32, name="identity")
+        make_identity(nc, identity[:])
+        turned = psum.tile([P, PACK, P], F32, name="turned")
+        by_feature = fk_row[:].rearrange("q (p t) -> q t p", t=PACK)
+        for t in range(PACK):
+            nc.tensor.transpose(turned[:, t, :], by_feature[:, t, :], identity[:])
+        factor = keep.tile([P, PACK], F32, name="factor")
+        size = keep.tile([P, PACK], F32, name="size")
+        sign = keep.tile([P, PACK], F32, name="sign")
+        nc.scalar.activation(out=size[:], in_=turned[:, :, fk_at], func=ACT.Abs)
+        nc.scalar.activation(out=sign[:], in_=turned[:, :, fk_at], func=ACT.Sign)
+        nc.scalar.copy(out=factor[:], in_=turned[:, :, fk_at])
+
         banks = [psum.tile([P, B], F32, name=f"bank{g}") for g in range(N // P)]
         for g in range(N // P):
             nc.tensor.matmul_mx(
@@ -79,11 +96,6 @@ def tile_moe_expert_heads_bundled_kernel(
                 start=True,
                 stop=False,
             )
-
-        size = keep.tile([P, PACK], F32, name="size")
-        sign = keep.tile([P, PACK], F32, name="sign")
-        nc.scalar.activation(out=size[:], in_=factor[:], func=ACT.Abs)
-        nc.scalar.activation(out=sign[:], in_=factor[:], func=ACT.Sign)
 
         u = keep.tile([P, B, PACK], BF16, name="u", align_bytes=64)
 

from contextlib import ExitStack

import concourse.mybir as mybir
from concourse.masks import make_identity

K, T, J, B, N = 512, 2048, 1024, 128, 512
P = 128
PACK = 4
BUNDLE = J // B
HALF_J = J // 2
HALF_B = B // 2
PER_COLUMN = 16
QUADRANTS = 4
FLOPS = 2 * 2 * K * N * B

F32 = mybir.dt.float32
BF16 = mybir.dt.bfloat16
I32 = mybir.dt.int32
U32 = mybir.dt.uint32
U16 = mybir.dt.uint16
U8 = mybir.dt.uint8
FP8X4 = mybir.dt.float8_e4m3fn_x4
FP4X4 = mybir.dt.float4_e2m1fn_x4
ALU = mybir.AluOpType
ACT = mybir.ActivationFunctionType


def load_scales(nc, tile, scales, quadrants):
    for q in quadrants:
        nc.sync.dma_start(
            out=tile[32 * q : 32 * q + 4, :].bitcast(I32),
            in_=scales[0, 4 * q : 4 * q + 4, :].bitcast(I32),
        )


def tile_moe_expert_heads_bundled_kernel(
    tc, xf, fk, w_words, w_scales, bx_words, bx_scales, wb_words, wb_scales, offs, out
):
    nc = tc.nc
    with ExitStack() as ctx:
        keep = ctx.enter_context(tc.tile_pool(name="keep", bufs=1))
        psum = ctx.enter_context(tc.psum_pool(name="psum", bufs=1))

        offsets = keep.tile([P, J // PER_COLUMN], U16, name="offsets")
        windows = [keep.tile([P, T], F32, name=f"window{t}") for t in range(PACK)]
        fk_row = keep.tile([P, K], F32, name="fk_row")
        w_codes = keep.tile([P, 2 * N], U8, name="w_codes", align_bytes=64)
        wb_codes = keep.tile([P, 2 * N], U8, name="wb_codes", align_bytes=64)
        bx_codes = keep.tile([P, PACK * B], U8, name="bx_codes", align_bytes=64)
        w_scale = keep.tile([P, N], U8, name="w_scale", align_bytes=64)
        wb_scale = keep.tile([P, N], U8, name="wb_scale", align_bytes=64)
        bx_scale = keep.tile([P, B], U8, name="bx_scale", align_bytes=64)

        fk_at = P - 1
        nc.scalar.dma_start(out=fk_row[fk_at:, :], in_=fk.rearrange("k o -> o k"))
        nc.vector.memset(fk_row[:fk_at, :], 0.0)

        rows = xf.rearrange("(p t) w -> p t w", t=PACK)
        nc.sync.dma_start(out=windows[0][:], in_=rows[:, 0, :])
        nc.sync.dma_start(offsets[:], offs)
        nc.sync.dma_start(out=windows[1][:], in_=rows[:, 1, :])
        nc.sync.dma_start(out=windows[2][:], in_=rows[:, 2, :])
        load_scales(nc, wb_scale, wb_scales, range(QUADRANTS))
        load_scales(nc, bx_scale, bx_scales, range(QUADRANTS // 2))
        nc.sync.dma_start(out=windows[3][:], in_=rows[:, 3, :])
        nc.sync.dma_start(out=wb_codes[:].bitcast(I32), in_=wb_words[0].bitcast(I32))
        nc.sync.dma_start(
            out=bx_codes[:].bitcast(I32),
            in_=bx_words[0].rearrange("p c r -> p (c r)").bitcast(I32),
        )
        nc.sync.dma_start(out=w_codes[:].bitcast(I32), in_=w_words[0].bitcast(I32))
        load_scales(nc, bx_scale, bx_scales, range(QUADRANTS // 2, QUADRANTS))
        load_scales(nc, w_scale, w_scales, range(QUADRANTS))

        identity = keep.tile([P, P], F32, name="identity")
        make_identity(nc, identity[:])
        turned = psum.tile([P, PACK, P], F32, name="turned")
        by_feature = fk_row[:].rearrange("q (p t) -> q t p", t=PACK)
        for t in range(PACK):
            nc.tensor.transpose(turned[:, t, :], by_feature[:, t, :], identity[:])
        factor = keep.tile([P, PACK], F32, name="factor")
        size = keep.tile([P, PACK], F32, name="size")
        sign = keep.tile([P, PACK], F32, name="sign")
        nc.scalar.activation(out=size[:], in_=turned[:, :, fk_at], func=ACT.Abs)
        nc.scalar.activation(out=sign[:], in_=turned[:, :, fk_at], func=ACT.Sign)
        nc.scalar.copy(out=factor[:], in_=turned[:, :, fk_at])

        banks = [psum.tile([P, B], F32, name=f"bank{g}") for g in range(N // P)]
        for g in range(N // P):
            nc.tensor.matmul_mx(
                out=banks[g][:],
                lhsT=wb_codes[:, 2 * P * g : 2 * P * (g + 1)].bitcast(FP4X4),
                lhsT_scale=wb_scale[:, P * g : P * (g + 1)],
                rhs=bx_codes[:].bitcast(FP8X4),
                rhs_scale=bx_scale[:],
                start=True,
                stop=False,
            )

        u = keep.tile([P, B, PACK], BF16, name="u", align_bytes=64)

        def gather(t, lo, hi):
            picked = keep.tile([P, hi - lo], F32, name=f"picked{t}_{lo}")
            entries = offsets[:, lo // PER_COLUMN : hi // PER_COLUMN]
            nc.vector.tensor_copy(picked[:], windows[t][:].indirect(entries))
            return picked

        def scale(dst, picked, t):
            nc.scalar.activation(
                out=dst.rearrange("p (c r e) -> p c r e", r=BUNDLE, e=2),
                in_=picked[:].rearrange("p (c e r) -> p c r e", r=BUNDLE, e=2),
                func=ACT.Copy,
                scale=size[:, t : t + 1],
            )

        def halve(dst, src, run):
            s = src.rearrange("p (c h w) -> p c h w", h=2, w=run)
            d = dst.rearrange("p (c w) -> p c w", w=run)
            nc.vector.tensor_tensor(out=d, in0=s[:, :, 0, :], in1=s[:, :, 1, :], op=ALU.max)

        def place(src, t, b0, by):
            width = src.shape[1]
            nc.scalar.activation(out=u[:, b0 : b0 + width, t], in_=src, func=ACT.Copy, scale=by[:, t : t + 1])

        def levels(label, slots, count):
            return [keep.tile([P, slots >> i], BF16, name=f"{label}{BUNDLE >> i}") for i in range(count)]

        half_lists = 5
        early8, early4, early2, early1 = levels("early", half_lists * HALF_J, 4)
        mid8, mid4, mid2 = levels("mid", HALF_J, 3)
        late8, late4, late2, late1 = levels("late", HALF_J, 4)

        def halve_early(dst, src, run, part):
            s = src[:].rearrange("p (n g c h w) -> p n g c h w", n=half_lists, g=2, h=2, w=run)[:, :, part]
            d = dst[:].rearrange("p (n g c w) -> p n g c w", n=half_lists, g=2, w=run)[:, :, part]
            nc.vector.tensor_tensor(out=d, in0=s[:, :, :, 0, :], in1=s[:, :, :, 1, :], op=ALU.max)

        for t in range(2):
            scale(early8[:, t * J : (t + 1) * J], gather(t, 0, J), t)
        scale(early8[:, 2 * J :], gather(2, 0, HALF_J), 2)
        scale(mid8[:], gather(2, HALF_J, J), 2)

        halve_early(early4, early8, 8, 0)
        halve_early(early4, early8, 8, 1)
        halve_early(early2, early4, 4, 0)
        halve(mid4[:], mid8[:], 8)
        halve_early(early2, early4, 4, 1)
        halve_early(early1, early2, 2, 0)
        halve(mid2[:], mid4[:], 4)
        halve_early(early1, early2, 2, 1)
        for t in range(2):
            place(early1[:, t * B : (t + 1) * B], t, 0, sign)
        place(early1[:, 2 * B :], 2, 0, sign)

        first = gather(3, 0, HALF_J)
        scale(late8[:], first, 3)
        last = gather(3, HALF_J, J)

        last1 = first[:, :HALF_B]
        mid1 = first[:, HALF_B:B]

        def reduce_last(lo, hi):
            nc.vector.tensor_reduce(
                out=last1[:, lo:hi],
                in_=last[:, lo * BUNDLE : hi * BUNDLE].rearrange("p (b r) -> p b r", r=BUNDLE),
                axis=mybir.AxisListType.X,
                op=ALU.max,
            )
            place(last1[:, lo:hi], 3, HALF_B + lo, factor)

        halve(late4[:], late8[:], 8)
        halve(mid1, mid2[:], 2)
        place(mid1, 2, HALF_B, sign)
        reduce_last(0, HALF_B // 2)
        halve(late2[:], late4[:], 4)
        reduce_last(HALF_B // 2, HALF_B)
        halve(late1[:], late2[:], 2)
        place(late1[:], 3, 0, sign)

        u_codes = keep.tile([P, B], U32, name="u_codes", align_bytes=64)
        u_scale = keep.tile([P, B], U8, name="u_scale", align_bytes=64)
        nc.vector.quantize_mx(
            out=u_codes[:].bitcast(FP8X4), scales=u_scale[:], in_=u[:].rearrange("p b t -> p (b t)")
        )

        for g in range(N // P):
            nc.tensor.matmul_mx(
                out=banks[g][:],
                lhsT=w_codes[:, 2 * P * g : 2 * P * (g + 1)].bitcast(FP4X4),
                lhsT_scale=w_scale[:, P * g : P * (g + 1)],
                rhs=u_codes[:].bitcast(FP8X4),
                rhs_scale=u_scale[:],
                start=False,
                stop=True,
            )
            result = keep.tile([P, B], F32, name=f"result{g}")
            if g % 2 == 0:
                nc.vector.tensor_copy(out=result[:], in_=banks[g][:])
                nc.sync.dma_start(out=out[P * g : P * (g + 1), :], in_=result[:])
            else:
                nc.scalar.copy(out=result[:], in_=banks[g][:])
                nc.scalar.dma_start(out=out[P * g : P * (g + 1), :], in_=result[:])
